import numpy as np
import ml_dtypes


def mxq(x, axis, fmt="e4m3"):
    dtype, down = {"e4m3": (ml_dtypes.float8_e4m3fn, 7), "e5m2": (ml_dtypes.float8_e5m2, 14)}[fmt]
    v = np.moveaxis(np.asarray(x, np.float32).astype(ml_dtypes.bfloat16).astype(np.float64), axis, -1)
    blocks = v.reshape(v.shape[:-1] + (-1, 32))
    amax = np.abs(blocks).max(-1, keepdims=True)
    byte = np.maximum(np.where(amax > 0, np.frexp(amax)[1] - 1 + 127, 0) - down, 1)
    scale = np.exp2(byte - 127.0)
    codes = (blocks / scale).astype(np.float32).astype(dtype).astype(np.float64)
    return np.moveaxis((codes * scale).reshape(v.shape), -1, axis)


WIDE = False


def mx_kscale(k):
    if not WIDE:
        return np.ones(k)
    levels = np.array([10, -10, 5, -5, 0])
    if k % 512:
        return np.exp2(np.random.permutation(np.resize(levels, k // 32))).repeat(32)
    a = np.empty((k // 512, 16))
    for p in range(k // 512):
        a[p, :8] = np.random.permutation(np.resize(levels, 8))
        for g in range(8):
            far = levels[np.abs(levels - a[p, g]) >= 10]
            a[p, g + 8] = far[np.random.randint(len(far))]
    return np.exp2(a.ravel()).repeat(32)


def f64(x):
    return np.asarray(x).astype(np.float64)


def striped(idx):
    return np.tile(idx.reshape(-1, 16).T, (8, 1)).astype(np.uint16)


def unstriped(offs):
    return offs[:16].T.reshape(-1).astype(np.int64)


def pack_weight(w):
    k, n = w.shape
    w = f64(np.asarray(w, np.float32).astype(ml_dtypes.bfloat16)).reshape(k // 32, 32, n)
    amax = np.abs(w).max(1)
    byte = np.clip(np.where(amax > 0, np.frexp(amax)[1] - 1 + 127 - 7, 1), 1, 254)
    scaled = (w * np.exp2(127.0 - byte)[:, None, :]).reshape(k, n).astype(np.float32)
    words = np.ascontiguousarray(scaled.reshape(k // 512, 128, 4, n).transpose(0, 1, 3, 2)).astype(ml_dtypes.float8_e4m3fn).view(np.uint8)
    return words, np.ascontiguousarray(byte.astype(np.uint8).reshape(k // 512, 16, n))


def unpack_weight(words, scales):
    g, p, n, _ = words.shape
    vals = np.ascontiguousarray(words).view(ml_dtypes.float8_e4m3fn).astype(np.float64) * np.repeat(np.exp2(scales.astype(np.float64) - 127.0), 8, axis=1)[..., None]
    return vals.transpose(0, 1, 3, 2).reshape(g * 512, n)


K, T, S, N, V, U = 1024, 2048, 512, 256, 256, 512
P = 2 ** 7


def setup_inputs():
    n = np.random.standard_normal
    s = mx_kscale(K)[:, None]
    packed_xT = pack_weight(n((K, T)) * s)
    return {
        "x_words": packed_xT[0],
        "x_scales": packed_xT[1],
        "w1": (n((K, N)) / np.sqrt(K) / s).astype(np.float32),
        "kern": (np.tile(np.random.uniform(0.1, 0.8, U), (P, 1))).astype(np.float32),
        "offs": striped(np.random.permutation(T)[:S]),
        "ba": striped(np.random.permutation(S)),
        "bb": striped(np.random.permutation(S)),
        "gaina": striped(np.random.permutation(U)[:V]),
        "gainb": striped(np.random.permutation(U)[:V]),
        "lossa": striped(np.random.permutation(U)[:V]),
        "who": striped(np.random.permutation(S)[:V]),
    }


def reference(x_words, x_scales, w1, kern, offs, ba, bb, gaina, gainb, lossa, who):
    xq = unpack_weight(x_words, x_scales)[:, unstriped(offs)]
    y = mxq(f64(w1), 0, "e4m3").T @ xq
    num = np.exp(0.6 * y)
    own = num[:, unstriped(who)]
    rate = (f64(kern)[:1] * num[:, unstriped(ba)]) * num[:, unstriped(bb)]
    gain = 0.5 * (rate[:, unstriped(gaina)] + rate[:, unstriped(gainb)])
    return (own + gain) / (rate[:, unstriped(lossa)] / (own + 0.2) + 1.0)

@@ -1,0 +1,148 @@
+import math
+from contextlib import ExitStack
+
+import concourse.mybir as mybir
+
+K, T, S, N, V = 1024, 2048, 512, 256, 256
+P = 128
+PACK = 4
+K_PASS = P * PACK
+PASSES = K // K_PASS
+M_TILES = N // P
+HALF = S // 2
+WIDE = 2048
+FLOPS = 2 * K * N * S
+
+F32 = mybir.dt.float32
+BF16 = mybir.dt.bfloat16
+I32 = mybir.dt.int32
+U32 = mybir.dt.uint32
+U16 = mybir.dt.uint16
+U8 = mybir.dt.uint8
+FP8X4 = mybir.dt.float8_e4m3fn_x4
+ACT = mybir.ActivationFunctionType
+MULT = mybir.AluOpType.mult
+ADD = mybir.AluOpType.add
+
+
+def tile_picked_ycoagu_imp_p_kernel(tc, x_words, x_scales, w1, kern, offs, ba, bb, gaina, gainb, lossa, who, out):
+    nc = tc.nc
+    with ExitStack() as ctx:
+        lists = ctx.enter_context(tc.tile_pool(name="lists", bufs=1))
+        sb = ctx.enter_context(tc.tile_pool(name="sb", bufs=1))
+        psum = ctx.enter_context(tc.psum_pool(name="psum", bufs=1))
+
+        def load_list(src, name):
+            t = lists.tile([P, src.shape[1]], U16, name=name)
+            nc.sync.dma_start(t[:], src)
+            return t
+
+        def f32(name, width):
+            return sb.tile([P, width], F32, name=name)
+
+        offs_t = load_list(offs, "offs_t")
+        x_sc = sb.tile([P, T], U8, name="x_sc", align_bytes=64)
+        nc.vector.memset(x_sc[:].bitcast(I32), 0)
+        x_w = [sb.tile([P, T], I32, name="x_w%d" % o) for o in range(PASSES)]
+        nc.sync.dma_start(x_w[0][:], x_words[0].rearrange("p c r -> p (c r)").bitcast(I32))
+        for q in range(4):
+            nc.sync.dma_start(x_sc[32 * q : 32 * q + 8, :].bitcast(I32), x_scales[:, 4 * q : 4 * q + 4, :].bitcast(I32))
+        w_raw0 = sb.tile([P, PACK, N], F32, name="w_raw0")
+        nc.sync.dma_start(w_raw0[:], w1[0:K_PASS, :].rearrange("(p j) m -> p j m", j=PACK))
+        w_raw1 = [sb.tile([P, PACK, P], F32, name="w_raw1%d" % m) for m in range(M_TILES)]
+
+        def load_w1(m):
+            nc.sync.dma_start(w_raw1[m][:], w1[K_PASS:K, m * P : (m + 1) * P].rearrange("(p j) m -> p j m", j=PACK))
+
+        load_w1(0)
+        nc.sync.dma_start(x_w[1][:], x_words[1].rearrange("p c r -> p (c r)").bitcast(I32))
+        load_w1(1)
+        ba_t = load_list(ba, "ba_t")
+        who_t = load_list(who, "who_t")
+        bb_t = load_list(bb, "bb_t")
+        kern_t = f32("kern_t", S)
+        nc.sync.dma_start(kern_t[:], kern)
+        lossa_t = load_list(lossa, "lossa_t")
+        gaina_t = load_list(gaina, "gaina_t")
+        gainb_t = load_list(gainb, "gainb_t")
+
+        y_win = [f32("y_win%d" % m, WIDE) for m in range(M_TILES)]
+        for m in range(M_TILES):
+            nc.gpsimd.memset(y_win[m][:, S:], 0.0)
+
+        def weave(name, raw, width):
+            g = sb.tile([P, width, PACK], BF16, name=name, align_bytes=64)
+            nc.scalar.copy(g[:].rearrange("p (c i) t -> p c t i", i=4), raw.rearrange("p t (c i) -> p c t i", i=4))
+            return g
+
+        def quantise(name, g, width):
+            codes = sb.tile([P, width], U32, name=name + "_c", align_bytes=64)
+            scales = sb.tile([P, width], U8, name=name + "_s", align_bytes=64)
+            nc.vector.quantize_mx(out=codes[:].bitcast(FP8X4), scales=scales[:], in_=g[:].rearrange("p w j -> p (w j)"))
+            return codes, scales
+
+        halves = [slice(0, HALF), slice(HALF, S)]
+        g_w = [sb.tile([P, S], U32, name="g_w%d" % o, align_bytes=64) for o in range(PASSES)]
+        g_sc = sb.tile([P, S], U8, name="g_sc", align_bytes=64)
+        nc.vector.tensor_copy(g_w[0][:], x_w[0][:].bitcast(U32).indirect(offs_t[:]))
+        nc.vector.tensor_copy(g_sc[:], x_sc[:].indirect(offs_t[:]))
+        wq0 = quantise("wq0", weave("wg0", w_raw0[:], N), N)
+        wq1 = [quantise("wq10", weave("wg10", w_raw1[0][:], P), P)]
+
+        acc = [[psum.tile([P, HALF], F32, name="acc%d%d" % (m, h)) for h in range(2)] for m in range(M_TILES)]
+        for m in range(M_TILES):
+            ms = slice(m * P, (m + 1) * P)
+            for h in range(2):
+                nc.tensor.matmul_mx(out=acc[m][h][:], lhsT=wq0[0][:, ms].bitcast(FP8X4), lhsT_scale=wq0[1][:, ms],
+                                    rhs=g_w[0][:, halves[h]].bitcast(FP8X4), rhs_scale=g_sc[:, halves[h]], start=True, stop=False)
+
+        def second_pass(m, h):
+            nc.tensor.matmul_mx(out=acc[m][h][:], lhsT=wq1[m][0][:].bitcast(FP8X4), lhsT_scale=wq1[m][1][:],
+                                rhs=g_w[1][:, halves[h]].bitcast(FP8X4), rhs_scale=g_sc[4:P, halves[h]], start=False, stop=True)
+
+        for h in range(2):
+            nc.vector.tensor_copy(g_w[1][:, halves[h]], x_w[1][:].bitcast(U32).indirect(offs_t[:, 16 * h : 16 * h + 16]))
+            second_pass(0, h)
+        wq1.append(quantise("wq11", weave("wg11", w_raw1[1][:], P), P))
+        for h in range(2):
+            second_pass(1, h)
+
+        ea = [f32("ea%d" % m, S) for m in range(M_TILES)]
+        eb = [f32("eb%d" % m, S) for m in range(M_TILES)]
+        ka = [f32("ka%d" % m, S) for m in range(M_TILES)]
+        rate = [f32("rate%d" % m, S) for m in range(M_TILES)]
+        yw = [f32("yw%d" % m, V) for m in range(M_TILES)]
+        own = [f32("own%d" % m, V) for m in range(M_TILES)]
+        ownh = [f32("ownh%d" % m, V) for m in range(M_TILES)]
+        den = [f32("den%d" % m, V) for m in range(M_TILES)]
+        n1 = [f32("n1%d" % m, V) for m in range(M_TILES)]
+        n2 = [f32("n2%d" % m, V) for m in range(M_TILES)]
+
+        nc.scalar.copy(y_win[0][:, halves[0]], acc[0][0][:])
+        nc.vector.tensor_copy(y_win[0][:, halves[1]], acc[0][1][:])
+        nc.vector.tensor_copy(yw[0][:], y_win[0][:].indirect(who_t[:]))
+        for h in range(2):
+            nc.vector.tensor_copy(y_win[1][:, halves[h]], acc[1][h][:])
+        nc.vector.tensor_copy(yw[1][:], y_win[1][:].indirect(who_t[:]))
+        for m in range(M_TILES):
+            nc.scalar.activation(ea[m][:], y_win[m][:].indirect(ba_t[:]), ACT.Exp, scale=0.6)
+            nc.scalar.activation(eb[m][:], y_win[m][:].indirect(bb_t[:]), ACT.Exp, scale=0.6)
+            nc.scalar.activation(ownh[m][:], yw[m][:], ACT.Exp, scale=0.6, bias=math.log(0.5))
+            nc.scalar.activation(own[m][:], yw[m][:], ACT.Exp, scale=0.6)
+        for m in range(M_TILES):
+            nc.vector.scalar_tensor_tensor(ka[m][:], ea[m][:], 0.5, kern_t[:], MULT, MULT)
+            nc.vector.tensor_tensor(rate[m][:], ka[m][:], eb[m][:], MULT)
+            nc.vector.tensor_tensor(den[m][:], rate[m][:].indirect(lossa_t[:]), ownh[m][:], ADD)
+            nc.vector.tensor_tensor(n1[m][:], rate[m][:].indirect(gaina_t[:]), own[m][:], ADD)
+            nc.vector.tensor_tensor(n2[m][:], rate[m][:].indirect(gainb_t[:]), n1[m][:], ADD)
+
+        for m in range(M_TILES):
+            root = sb.tile([P, V], F32, name="root", tag="yw1")
+            nc.scalar.activation(root[:], den[m][:], ACT.Abs_reciprocal_sqrt, bias=0.1)
+            inv = f32("inv%d" % m, V)
+            nc.scalar.activation(inv[:], root[:], ACT.Square)
+            share = f32("share%d" % m, V)
+            nc.vector.scalar_tensor_tensor(share[:], ownh[m][:], 0.1, inv[:], ADD, MULT)
+            res = f32("res%d" % m, V)
+            nc.vector.tensor_tensor(res[:], share[:], n2[m][:], MULT)
+            nc.sync.dma_start(out[m * P : (m + 1) * P, :], res[:])

@@ -11,6 +11,7 @@ PASSES = K // K_PASS
 M_TILES = N // P
 HALF = S // 2
 WIDE = 2048
+SPARE = 16
 FLOPS = 2 * K * N * S
 
 F32 = mybir.dt.float32
@@ -42,107 +43,131 @@ def tile_picked_ycoagu_imp_p_kernel(tc, x_words, x_scales, w1, kern, offs, ba, b
 
         offs_t = load_list(offs, "offs_t")
         x_sc = sb.tile([P, T], U8, name="x_sc", align_bytes=64)
-        nc.vector.memset(x_sc[:].bitcast(I32), 0)
-        x_w = [sb.tile([P, T], I32, name="x_w%d" % o) for o in range(PASSES)]
-        nc.sync.dma_start(x_w[0][:], x_words[0].rearrange("p c r -> p (c r)").bitcast(I32))
+        nc.gpsimd.memset(x_sc[:].bitcast(I32), 0)
         for q in range(4):
-            nc.sync.dma_start(x_sc[32 * q : 32 * q + 8, :].bitcast(I32), x_scales[:, 4 * q : 4 * q + 4, :].bitcast(I32))
-        w_raw0 = sb.tile([P, PACK, N], F32, name="w_raw0")
-        nc.sync.dma_start(w_raw0[:], w1[0:K_PASS, :].rearrange("(p j) m -> p j m", j=PACK))
-        w_raw1 = [sb.tile([P, PACK, P], F32, name="w_raw1%d" % m) for m in range(M_TILES)]
+            queue = nc.scalar if q < 2 else nc.gpsimd
+            queue.dma_start(x_sc[32 * q : 32 * q + 8, :].bitcast(I32), x_scales[:, 4 * q : 4 * q + 4, :].bitcast(I32))
+        x_w = [sb.tile([P, T], I32, name="x_w%d" % o, align_bytes=64) for o in range(PASSES)]
+        y_win = [f32("y_win%d" % m, WIDE) for m in range(M_TILES)]
+        late = f32("late", PACK * P)
+        w_raw = [
+            y_win[0][:, S : S + PACK * N].rearrange("p (j m) -> p j m", j=PACK),
+            y_win[1][:, S : S + PACK * P].rearrange("p (j m) -> p j m", j=PACK),
+            late[:].rearrange("p (j m) -> p j m", j=PACK),
+        ]
 
-        def load_w1(m):
-            nc.sync.dma_start(w_raw1[m][:], w1[K_PASS:K, m * P : (m + 1) * P].rearrange("(p j) m -> p j m", j=PACK))
+        def load_words(o):
+            nc.sync.dma_start(x_w[o][:], x_words[o].rearrange("p c r -> p (c r)").bitcast(I32))
 
-        load_w1(0)
-        nc.sync.dma_start(x_w[1][:], x_words[1].rearrange("p c r -> p (c r)").bitcast(I32))
-        load_w1(1)
-        ba_t = load_list(ba, "ba_t")
-        who_t = load_list(who, "who_t")
+        load_words(0)
+        nc.sync.dma_start(w_raw[0], w1[0:K_PASS, :].rearrange("(p j) m -> p j m", j=PACK))
+        nc.sync.dma_start(w_raw[1], w1[K_PASS:K, 0:P].rearrange("(p j) m -> p j m", j=PACK))
+        load_words(1)
+        nc.sync.dma_start(w_raw[2], w1[K_PASS:K, P:N].rearrange("(p j) m -> p j m", j=PACK))
         bb_t = load_list(bb, "bb_t")
         kern_t = f32("kern_t", S)
         nc.sync.dma_start(kern_t[:], kern)
-        lossa_t = load_list(lossa, "lossa_t")
+        ba_t = load_list(ba, "ba_t")
+        who_t = load_list(who, "who_t")
         gaina_t = load_list(gaina, "gaina_t")
+        lossa_t = load_list(lossa, "lossa_t")
         gainb_t = load_list(gainb, "gainb_t")
+        num0 = f32("num0", S + SPARE)
+        nc.vector.memset(num0[:, S:], 0.0)
+        nc.vector.memset(y_win[0][:, WIDE - S :], 0.0)
 
-        y_win = [f32("y_win%d" % m, WIDE) for m in range(M_TILES)]
-        for m in range(M_TILES):
-            nc.gpsimd.memset(y_win[m][:, S:], 0.0)
-
-        def weave(name, raw, width):
-            g = sb.tile([P, width, PACK], BF16, name=name, align_bytes=64)
-            nc.scalar.copy(g[:].rearrange("p (c i) t -> p c t i", i=4), raw.rearrange("p t (c i) -> p c t i", i=4))
-            return g
-
-        def quantise(name, g, width):
-            codes = sb.tile([P, width], U32, name=name + "_c", align_bytes=64)
-            scales = sb.tile([P, width], U8, name=name + "_s", align_bytes=64)
+        def quantise(name, raw, width, copy):
+            g = sb.tile([P, width, PACK], BF16, name="wg" + name, align_bytes=64)
+            copy(g[:].rearrange("p (c i) t -> p c t i", i=4), raw.rearrange("p t (c i) -> p c t i", i=4))
+            codes = sb.tile([P, width], U32, name="wc" + name, align_bytes=64)
+            scales = sb.tile([P, width], U8, name="ws" + name, align_bytes=64)
             nc.vector.quantize_mx(out=codes[:].bitcast(FP8X4), scales=scales[:], in_=g[:].rearrange("p w j -> p (w j)"))
             return codes, scales
 
         halves = [slice(0, HALF), slice(HALF, S)]
+        acc0 = [psum.tile([P, HALF], F32, name="acc0%d" % h) for h in range(2)]
+        acc1 = psum.tile([P, S], F32, name="acc1")
         g_w = [sb.tile([P, S], U32, name="g_w%d" % o, align_bytes=64) for o in range(PASSES)]
-        g_sc = sb.tile([P, S], U8, name="g_sc", align_bytes=64)
+
+        def picked(h):
+            return offs_t[:, 16 * h : 16 * h + 16]
+
+        def product(acc, o, codes, scales, cols):
+            nc.tensor.matmul_mx(out=acc[:], lhsT=codes.bitcast(FP8X4), lhsT_scale=scales,
+                                rhs=g_w[o][:, cols].bitcast(FP8X4), rhs_scale=g_sc[4 * o : P, cols],
+                                start=(o == 0), stop=(o == PASSES - 1))
+
         nc.vector.tensor_copy(g_w[0][:], x_w[0][:].bitcast(U32).indirect(offs_t[:]))
+        g_sc = sb.tile([P, S], U8, name="g_sc", tag="x_w0", align_bytes=64)
         nc.vector.tensor_copy(g_sc[:], x_sc[:].indirect(offs_t[:]))
-        wq0 = quantise("wq0", weave("wg0", w_raw0[:], N), N)
-        wq1 = [quantise("wq10", weave("wg10", w_raw1[0][:], P), P)]
-
-        acc = [[psum.tile([P, HALF], F32, name="acc%d%d" % (m, h)) for h in range(2)] for m in range(M_TILES)]
-        for m in range(M_TILES):
-            ms = slice(m * P, (m + 1) * P)
-            for h in range(2):
-                nc.tensor.matmul_mx(out=acc[m][h][:], lhsT=wq0[0][:, ms].bitcast(FP8X4), lhsT_scale=wq0[1][:, ms],
-                                    rhs=g_w[0][:, halves[h]].bitcast(FP8X4), rhs_scale=g_sc[:, halves[h]], start=True, stop=False)
-
-        def second_pass(m, h):
-            nc.tensor.matmul_mx(out=acc[m][h][:], lhsT=wq1[m][0][:].bitcast(FP8X4), lhsT_scale=wq1[m][1][:],
-                                rhs=g_w[1][:, halves[h]].bitcast(FP8X4), rhs_scale=g_sc[4:P, halves[h]], start=False, stop=True)
-
+        wc0, ws0 = quantise("0", w_raw[0], N, nc.scalar.copy)
         for h in range(2):
-            nc.vector.tensor_copy(g_w[1][:, halves[h]], x_w[1][:].bitcast(U32).indirect(offs_t[:, 16 * h : 16 * h + 16]))
-            second_pass(0, h)
-        wq1.append(quantise("wq11", weave("wg11", w_raw1[1][:], P), P))
+            product(acc0[h], 0, wc0[:, 0:P], ws0[:, 0:P], halves[h])
+        product(acc1, 0, wc0[:, P:N], ws0[:, P:N], slice(0, S))
+        wc10, ws10 = quantise("10", w_raw[1], P, nc.scalar.copy)
         for h in range(2):
-            second_pass(1, h)
+            nc.vector.tensor_copy(g_w[1][:, halves[h]], x_w[1][:].bitcast(U32).indirect(picked(h)))
+            product(acc0[h], 1, wc10[:], ws10[:], halves[h])
+        wc11, ws11 = quantise("11", w_raw[2], P, nc.vector.tensor_copy)
+        product(acc1, 1, wc11[:], ws11[:], slice(0, S))
 
-        ea = [f32("ea%d" % m, S) for m in range(M_TILES)]
-        eb = [f32("eb%d" % m, S) for m in range(M_TILES)]
-        ka = [f32("ka%d" % m, S) for m in range(M_TILES)]
+        ea1 = f32("ea1", S)
+        ea = [y_win[1][:, WIDE - S :], ea1[:]]
+        eb1 = f32("eb1", S)
+        kb1 = f32("kb1", S)
+        kb = [y_win[1][:, 2 * S : 3 * S], kb1[:]]
         rate = [f32("rate%d" % m, S) for m in range(M_TILES)]
-        yw = [f32("yw%d" % m, V) for m in range(M_TILES)]
+        yw1 = f32("yw1", V)
         own = [f32("own%d" % m, V) for m in range(M_TILES)]
         ownh = [f32("ownh%d" % m, V) for m in range(M_TILES)]
         den = [f32("den%d" % m, V) for m in range(M_TILES)]
         n1 = [f32("n1%d" % m, V) for m in range(M_TILES)]
         n2 = [f32("n2%d" % m, V) for m in range(M_TILES)]
+        inv = [f32("inv%d" % m, V) for m in range(M_TILES)]
+        share = [f32("share%d" % m, V) for m in range(M_TILES)]
+        res = [f32("res%d" % m, V) for m in range(M_TILES)]
 
-        nc.scalar.copy(y_win[0][:, halves[0]], acc[0][0][:])
-        nc.vector.tensor_copy(y_win[0][:, halves[1]], acc[0][1][:])
-        nc.vector.tensor_copy(yw[0][:], y_win[0][:].indirect(who_t[:]))
-        for h in range(2):
-            nc.vector.tensor_copy(y_win[1][:, halves[h]], acc[1][h][:])
-        nc.vector.tensor_copy(yw[1][:], y_win[1][:].indirect(who_t[:]))
-        for m in range(M_TILES):
-            nc.scalar.activation(ea[m][:], y_win[m][:].indirect(ba_t[:]), ACT.Exp, scale=0.6)
-            nc.scalar.activation(eb[m][:], y_win[m][:].indirect(bb_t[:]), ACT.Exp, scale=0.6)
-            nc.scalar.activation(ownh[m][:], yw[m][:], ACT.Exp, scale=0.6, bias=math.log(0.5))
-            nc.scalar.activation(own[m][:], yw[m][:], ACT.Exp, scale=0.6)
-        for m in range(M_TILES):
-            nc.vector.scalar_tensor_tensor(ka[m][:], ea[m][:], 0.5, kern_t[:], MULT, MULT)
-            nc.vector.tensor_tensor(rate[m][:], ka[m][:], eb[m][:], MULT)
-            nc.vector.tensor_tensor(den[m][:], rate[m][:].indirect(lossa_t[:]), ownh[m][:], ADD)
-            nc.vector.tensor_tensor(n1[m][:], rate[m][:].indirect(gaina_t[:]), own[m][:], ADD)
-            nc.vector.tensor_tensor(n2[m][:], rate[m][:].indirect(gainb_t[:]), n1[m][:], ADD)
+        def fetch_add(dst, m, lst, other):
+            nc.vector.tensor_tensor(dst[m][:], rate[m][:].indirect(lst[:]), other[m][:], ADD)
 
-        for m in range(M_TILES):
+        def invert(m):
             root = sb.tile([P, V], F32, name="root", tag="yw1")
             nc.scalar.activation(root[:], den[m][:], ACT.Abs_reciprocal_sqrt, bias=0.1)
-            inv = f32("inv%d" % m, V)
-            nc.scalar.activation(inv[:], root[:], ACT.Square)
-            share = f32("share%d" % m, V)
-            nc.vector.scalar_tensor_tensor(share[:], ownh[m][:], 0.1, inv[:], ADD, MULT)
-            res = f32("res%d" % m, V)
-            nc.vector.tensor_tensor(res[:], share[:], n2[m][:], MULT)
-            nc.sync.dma_start(out[m * P : (m + 1) * P, :], res[:])
+            nc.scalar.activation(inv[m][:], root[:], ACT.Square)
+
+        def weigh(m):
+            nc.vector.scalar_tensor_tensor(share[m][:], ownh[m][:], 0.1, inv[m][:], ADD, MULT)
+
+        def finish(m):
+            nc.vector.tensor_tensor(res[m][:], share[m][:], n2[m][:], MULT)
+            nc.sync.dma_start(out[m * P : (m + 1) * P, :], res[m][:])
+
+        nc.scalar.activation(num0[:, halves[0]], acc0[0][:], ACT.Exp, scale=0.6)
+        nc.scalar.copy(y_win[0][:, halves[0]], acc0[0][:])
+        nc.scalar.activation(num0[:, halves[1]], acc0[1][:], ACT.Exp, scale=0.6)
+        nc.scalar.copy(y_win[0][:, halves[1]], acc0[1][:])
+        nc.scalar.activation(ea[0], y_win[0][:].indirect(ba_t[:]), ACT.Exp, scale=0.6)
+        nc.vector.tensor_tensor(kb[0], num0[:].indirect(bb_t[:]), kern_t[:], MULT)
+        nc.vector.tensor_copy(own[0][:], num0[:, 0:S].indirect(who_t[:]))
+        nc.scalar.copy(y_win[1][:, 0:S], acc1[:])
+        nc.vector.scalar_tensor_tensor(rate[0][:], kb[0], 0.5, ea[0], MULT, MULT)
+        nc.scalar.activation(ownh[0][:], own[0][:], ACT.Copy, scale=0.5)
+        nc.vector.tensor_copy(yw1[:], y_win[1][:, 0:S].indirect(who_t[:]))
+        nc.scalar.activation(ea[1], y_win[1][:].indirect(ba_t[:]), ACT.Exp, scale=0.6)
+        nc.scalar.activation(eb1[:], y_win[1][:].indirect(bb_t[:]), ACT.Exp, scale=0.6)
+        nc.scalar.activation(ownh[1][:], yw1[:], ACT.Exp, scale=0.6, bias=math.log(0.5))
+        nc.scalar.activation(own[1][:], yw1[:], ACT.Exp, scale=0.6)
+        fetch_add(n1, 0, gaina_t, own)
+        nc.vector.scalar_tensor_tensor(kb[1], ea[1], 0.5, kern_t[:], MULT, MULT)
+        fetch_add(den, 0, lossa_t, ownh)
+        nc.vector.tensor_tensor(rate[1][:], kb[1], eb1[:], MULT)
+        fetch_add(n2, 0, gainb_t, n1)
+        fetch_add(den, 1, lossa_t, ownh)
+        fetch_add(n1, 1, gaina_t, own)
+        invert(0)
+        invert(1)
+        weigh(0)
+        fetch_add(n2, 1, gainb_t, n1)
+        weigh(1)
+        finish(0)
+        finish(1)

@@ -41,12 +41,8 @@ def tile_picked_ycoagu_imp_p_kernel(tc, x_words, x_scales, w1, kern, offs, ba, b
         def f32(name, width):
             return sb.tile([P, width], F32, name=name)
 
-        offs_t = load_list(offs, "offs_t")
         x_sc = sb.tile([P, T], U8, name="x_sc", align_bytes=64)
         nc.gpsimd.memset(x_sc[:].bitcast(I32), 0)
-        for q in range(4):
-            queue = nc.scalar if q < 2 else nc.gpsimd
-            queue.dma_start(x_sc[32 * q : 32 * q + 8, :].bitcast(I32), x_scales[:, 4 * q : 4 * q + 4, :].bitcast(I32))
         x_w = [sb.tile([P, T], I32, name="x_w%d" % o, align_bytes=64) for o in range(PASSES)]
         y_win = [f32("y_win%d" % m, WIDE) for m in range(M_TILES)]
         late = f32("late", PACK * P)
@@ -60,6 +56,9 @@ def tile_picked_ycoagu_imp_p_kernel(tc, x_words, x_scales, w1, kern, offs, ba, b
             nc.sync.dma_start(x_w[o][:], x_words[o].rearrange("p c r -> p (c r)").bitcast(I32))
 
         load_words(0)
+        offs_t = load_list(offs, "offs_t")
+        for q in range(4):
+            nc.sync.dma_start(x_sc[32 * q : 32 * q + 8, :].bitcast(I32), x_scales[:, 4 * q : 4 * q + 4, :].bitcast(I32))
         nc.sync.dma_start(w_raw[0], w1[0:K_PASS, :].rearrange("(p j) m -> p j m", j=PACK))
         nc.sync.dma_start(w_raw[1], w1[K_PASS:K, 0:P].rearrange("(p j) m -> p j m", j=PACK))
         load_words(1)
@@ -130,11 +129,6 @@ def tile_picked_ycoagu_imp_p_kernel(tc, x_words, x_scales, w1, kern, offs, ba, b
         def fetch_add(dst, m, lst, other):
             nc.vector.tensor_tensor(dst[m][:], rate[m][:].indirect(lst[:]), other[m][:], ADD)
 
-        def invert(m):
-            root = sb.tile([P, V], F32, name="root", tag="yw1")
-            nc.scalar.activation(root[:], den[m][:], ACT.Abs_reciprocal_sqrt, bias=0.1)
-            nc.scalar.activation(inv[m][:], root[:], ACT.Square)
-
         def weigh(m):
             nc.vector.scalar_tensor_tensor(share[m][:], ownh[m][:], 0.1, inv[m][:], ADD, MULT)
 
@@ -161,13 +155,17 @@ def tile_picked_ycoagu_imp_p_kernel(tc, x_words, x_scales, w1, kern, offs, ba, b
         nc.vector.scalar_tensor_tensor(kb[1], ea[1], 0.5, kern_t[:], MULT, MULT)
         fetch_add(den, 0, lossa_t, ownh)
         nc.vector.tensor_tensor(rate[1][:], kb[1], eb1[:], MULT)
-        fetch_add(n2, 0, gainb_t, n1)
         fetch_add(den, 1, lossa_t, ownh)
         fetch_add(n1, 1, gaina_t, own)
-        invert(0)
-        invert(1)
-        weigh(0)
+        root0 = sb.tile([P, V], F32, name="root0", tag="yw1")
+        root = [root0, f32("root1", V)]
+        for m in range(M_TILES):
+            nc.scalar.activation(root[m][:], den[m][:], ACT.Abs_reciprocal_sqrt, bias=0.1)
+        for m in range(M_TILES):
+            nc.scalar.activation(inv[m][:], root[m][:], ACT.Square)
+        fetch_add(n2, 0, gainb_t, n1)
         fetch_add(n2, 1, gainb_t, n1)
+        weigh(0)
         weigh(1)
         finish(0)
         finish(1)

import math
from contextlib import ExitStack

import concourse.mybir as mybir

K, T, S, N, V = 1024, 2048, 512, 256, 256
P = 128
PACK = 4
K_PASS = P * PACK
PASSES = K // K_PASS
M_TILES = N // P
HALF = S // 2
WIDE = 2048
SPARE = 16
FLOPS = 2 * K * N * S

F32 = mybir.dt.float32
BF16 = mybir.dt.bfloat16
I32 = mybir.dt.int32
U32 = mybir.dt.uint32
U16 = mybir.dt.uint16
U8 = mybir.dt.uint8
FP8X4 = mybir.dt.float8_e4m3fn_x4
ACT = mybir.ActivationFunctionType
MULT = mybir.AluOpType.mult
ADD = mybir.AluOpType.add


def tile_picked_ycoagu_imp_p_kernel(tc, x_words, x_scales, w1, kern, offs, ba, bb, gaina, gainb, lossa, who, out):
    nc = tc.nc
    with ExitStack() as ctx:
        lists = ctx.enter_context(tc.tile_pool(name="lists", bufs=1))
        sb = ctx.enter_context(tc.tile_pool(name="sb", bufs=1))
        psum = ctx.enter_context(tc.psum_pool(name="psum", bufs=1))

        def load_list(src, name):
            t = lists.tile([P, src.shape[1]], U16, name=name)
            nc.sync.dma_start(t[:], src)
            return t

        def f32(name, width):
            return sb.tile([P, width], F32, name=name)

        x_sc = sb.tile([P, T], U8, name="x_sc", align_bytes=64)
        nc.gpsimd.memset(x_sc[:].bitcast(I32), 0)
        x_w = [sb.tile([P, T], I32, name="x_w%d" % o, align_bytes=64) for o in range(PASSES)]
        y_win = [f32("y_win%d" % m, WIDE) for m in range(M_TILES)]
        late = f32("late", PACK * P)
        w_raw = [
            y_win[0][:, S : S + PACK * N].rearrange("p (j m) -> p j m", j=PACK),
            y_win[1][:, S : S + PACK * P].rearrange("p (j m) -> p j m", j=PACK),
            late[:].rearrange("p (j m) -> p j m", j=PACK),
        ]

        def load_words(o):
            nc.sync.dma_start(x_w[o][:], x_words[o].rearrange("p c r -> p (c r)").bitcast(I32))

        load_words(0)
        offs_t = load_list(offs, "offs_t")
        for q in range(4):
            nc.sync.dma_start(x_sc[32 * q : 32 * q + 8, :].bitcast(I32), x_scales[:, 4 * q : 4 * q + 4, :].bitcast(I32))
        nc.sync.dma_start(w_raw[0], w1[0:K_PASS, :].rearrange("(p j) m -> p j m", j=PACK))
        nc.sync.dma_start(w_raw[1], w1[K_PASS:K, 0:P].rearrange("(p j) m -> p j m", j=PACK))
        load_words(1)
        nc.sync.dma_start(w_raw[2], w1[K_PASS:K, P:N].rearrange("(p j) m -> p j m", j=PACK))
        bb_t = load_list(bb, "bb_t")
        kern_t = f32("kern_t", S)
        nc.sync.dma_start(kern_t[:], kern)
        ba_t = load_list(ba, "ba_t")
        who_t = load_list(who, "who_t")
        gaina_t = load_list(gaina, "gaina_t")
        lossa_t = load_list(lossa, "lossa_t")
        gainb_t = load_list(gainb, "gainb_t")
        num0 = f32("num0", S + SPARE)
        nc.vector.memset(num0[:, S:], 0.0)
        nc.vector.memset(y_win[0][:, WIDE - S :], 0.0)

        def quantise(name, raw, width, copy):
            g = sb.tile([P, width, PACK], BF16, name="wg" + name, align_bytes=64)
            copy(g[:].rearrange("p (c i) t -> p c t i", i=4), raw.rearrange("p t (c i) -> p c t i", i=4))
            codes = sb.tile([P, width], U32, name="wc" + name, align_bytes=64)
            scales = sb.tile([P, width], U8, name="ws" + name, align_bytes=64)
            nc.vector.quantize_mx(out=codes[:].bitcast(FP8X4), scales=scales[:], in_=g[:].rearrange("p w j -> p (w j)"))
            return codes, scales

        halves = [slice(0, HALF), slice(HALF, S)]
        acc0 = [psum.tile([P, HALF], F32, name="acc0%d" % h) for h in range(2)]
        acc1 = psum.tile([P, S], F32, name="acc1")
        g_w = [sb.tile([P, S], U32, name="g_w%d" % o, align_bytes=64) for o in range(PASSES)]

        def picked(h):
            return offs_t[:, 16 * h : 16 * h + 16]

        def product(acc, o, codes, scales, cols):
            nc.tensor.matmul_mx(out=acc[:], lhsT=codes.bitcast(FP8X4), lhsT_scale=scales,
                                rhs=g_w[o][:, cols].bitcast(FP8X4), rhs_scale=g_sc[4 * o : P, cols],
                                start=(o == 0), stop=(o == PASSES - 1))

        nc.vector.tensor_copy(g_w[0][:], x_w[0][:].bitcast(U32).indirect(offs_t[:]))
        g_sc = sb.tile([P, S], U8, name="g_sc", tag="x_w0", align_bytes=64)
        nc.vector.tensor_copy(g_sc[:], x_sc[:].indirect(offs_t[:]))
        wc0, ws0 = quantise("0", w_raw[0], N, nc.scalar.copy)
        for h in range(2):
            product(acc0[h], 0, wc0[:, 0:P], ws0[:, 0:P], halves[h])
        product(acc1, 0, wc0[:, P:N], ws0[:, P:N], slice(0, S))
        wc10, ws10 = quantise("10", w_raw[1], P, nc.scalar.copy)
        for h in range(2):
            nc.vector.tensor_copy(g_w[1][:, halves[h]], x_w[1][:].bitcast(U32).indirect(picked(h)))
            product(acc0[h], 1, wc10[:], ws10[:], halves[h])
        wc11, ws11 = quantise("11", w_raw[2], P, nc.vector.tensor_copy)
        product(acc1, 1, wc11[:], ws11[:], slice(0, S))

        ea1 = f32("ea1", S)
        ea = [y_win[1][:, WIDE - S :], ea1[:]]
        eb1 = f32("eb1", S)
        kb1 = f32("kb1", S)
        kb = [y_win[1][:, 2 * S : 3 * S], kb1[:]]
        rate = [f32("rate%d" % m, S) for m in range(M_TILES)]
        yw1 = f32("yw1", V)
        own = [f32("own%d" % m, V) for m in range(M_TILES)]
        ownh = [f32("ownh%d" % m, V) for m in range(M_TILES)]
        den = [f32("den%d" % m, V) for m in range(M_TILES)]
        n1 = [f32("n1%d" % m, V) for m in range(M_TILES)]
        n2 = [f32("n2%d" % m, V) for m in range(M_TILES)]
        inv = [f32("inv%d" % m, V) for m in range(M_TILES)]
        share = [f32("share%d" % m, V) for m in range(M_TILES)]
        res = [f32("res%d" % m, V) for m in range(M_TILES)]

        def fetch_add(dst, m, lst, other):
            nc.vector.tensor_tensor(dst[m][:], rate[m][:].indirect(lst[:]), other[m][:], ADD)

        def weigh(m):
            nc.vector.scalar_tensor_tensor(share[m][:], ownh[m][:], 0.1, inv[m][:], ADD, MULT)

        def finish(m):
            nc.vector.tensor_tensor(res[m][:], share[m][:], n2[m][:], MULT)
            nc.sync.dma_start(out[m * P : (m + 1) * P, :], res[m][:])

        nc.scalar.activation(num0[:, halves[0]], acc0[0][:], ACT.Exp, scale=0.6)
        nc.scalar.copy(y_win[0][:, halves[0]], acc0[0][:])
        nc.scalar.activation(num0[:, halves[1]], acc0[1][:], ACT.Exp, scale=0.6)
        nc.scalar.copy(y_win[0][:, halves[1]], acc0[1][:])
        nc.scalar.activation(ea[0], y_win[0][:].indirect(ba_t[:]), ACT.Exp, scale=0.6)
        nc.vector.tensor_tensor(kb[0], num0[:].indirect(bb_t[:]), kern_t[:], MULT)
        nc.vector.tensor_copy(own[0][:], num0[:, 0:S].indirect(who_t[:]))
        nc.scalar.copy(y_win[1][:, 0:S], acc1[:])
        nc.vector.scalar_tensor_tensor(rate[0][:], kb[0], 0.5, ea[0], MULT, MULT)
        nc.scalar.activation(ownh[0][:], own[0][:], ACT.Copy, scale=0.5)
        nc.vector.tensor_copy(yw1[:], y_win[1][:, 0:S].indirect(who_t[:]))
        nc.scalar.activation(ea[1], y_win[1][:].indirect(ba_t[:]), ACT.Exp, scale=0.6)
        nc.scalar.activation(eb1[:], y_win[1][:].indirect(bb_t[:]), ACT.Exp, scale=0.6)
        nc.scalar.activation(ownh[1][:], yw1[:], ACT.Exp, scale=0.6, bias=math.log(0.5))
        nc.scalar.activation(own[1][:], yw1[:], ACT.Exp, scale=0.6)
        fetch_add(n1, 0, gaina_t, own)
        nc.vector.scalar_tensor_tensor(kb[1], ea[1], 0.5, kern_t[:], MULT, MULT)
        fetch_add(den, 0, lossa_t, ownh)
        nc.vector.tensor_tensor(rate[1][:], kb[1], eb1[:], MULT)
        fetch_add(den, 1, lossa_t, ownh)
        fetch_add(n1, 1, gaina_t, own)
        root0 = sb.tile([P, V], F32, name="root0", tag="yw1")
        root = [root0, f32("root1", V)]
        for m in range(M_TILES):
            nc.scalar.activation(root[m][:], den[m][:], ACT.Abs_reciprocal_sqrt, bias=0.1)
        for m in range(M_TILES):
            nc.scalar.activation(inv[m][:], root[m][:], ACT.Square)
        fetch_add(n2, 0, gainb_t, n1)
        fetch_add(n2, 1, gainb_t, n1)
        weigh(0)
        weigh(1)
        finish(0)
        finish(1)
